import numpy as np, ml_dtypes
CORES = [50,52,122,124]
N = 4
KT, HT, TK = 2, 2, 64
def setup_inputs(rng):
    w = (rng.standard_normal((128, KT * HT * 128), dtype=np.float32) / 8).astype(ml_dtypes.bfloat16)
    return {"x": rng.standard_normal((N, 128, KT * TK), dtype=np.float32).astype(ml_dtypes.bfloat16), "w": np.broadcast_to(w, (N,) + w.shape).copy()}
def setup_inputs_big(rng):
    d = setup_inputs(rng)
    for k in ("x", "w"): d[k] = (d[k].astype(np.float32) * 1024.0).astype(d[k].dtype)
    return d
def setup_inputs_small(rng):
    d = setup_inputs(rng)
    for k in ("x", "w"): d[k] = (d[k].astype(np.float32) * (1 / 1024.0)).astype(d[k].dtype)
    return d
def setup_inputs_apart(rng):
    d = setup_inputs(rng)
    f = (10.0 ** rng.permutation(np.linspace(-1.5, 1.5, N))).astype(np.float32).reshape(N, 1, 1)
    for k in ("x",): d[k] = (d[k].astype(np.float32) * f).astype(d[k].dtype)
    return d
def tie_inputs(x):
    x = dict(x)
    x["w"] = np.broadcast_to(x["w"][0], x["w"].shape).copy()
    return x
def reference(x, w):
    X, W = x.astype(np.float64), w.astype(np.float64)
    def hidden(r):
        return np.stack([np.maximum(sum(W[r][:, 128 * (HT * t + u):128 * (HT * t + u) + 128].T @ X[r][:, TK * t:TK * t + TK] for t in range(KT)), 0.0) for u in range(HT)])
    h = [hidden(r) for r in range(N)]
    y = np.stack([sum(h[(r - 1) % N][u].T @ h[r][u] for u in range(HT)) for r in range(N)])
    return {"y": y.astype(ml_dtypes.bfloat16 if x.dtype != np.float64 else np.float64)}

from concourse.mybir import AluOpType

TK = 64
KT, HT = 2, 2

SCRATCH = {
    "xs": ("sbuf", [128, 128], "bfloat16"),
    "ws": ("sbuf", [128, 512], "bfloat16"),
    "xp": ("sbuf", [128, 128], "bfloat16"),
    "hr": ("sbuf", [128, 128], "bfloat16"),
    "hp": ("sbuf", [128, 128], "bfloat16"),
    "zero": ("sbuf", [128, 128], "float32"),
    "ys": ("sbuf", [128, 64], "bfloat16"),
    "xd": ("dram", [128, 128], "bfloat16"),
    "xr": ("dram", [128, 128], "bfloat16"),
    "po": ("psum", [128, 512], "float32"),
    "pp0": ("psum", [128, 512], "float32"),
    "pp1": ("psum", [128, 512], "float32"),
    "py": ("psum", [128, 512], "float32"),
}
SEMAPHORES = ["ldd", "ldx", "ldw", "hand", "arr", "sent", "zs", "po_done", "hr_done", "pp0_done", "pp1_done",
              "hp0_done", "hp1_done", "py_done", "ys_done", "sty"]

K_LAND = 8
K_HAND = 4


def _pick(mask, k):
    bits = [i for i in range(16) if (mask >> i) & 1]
    k = min(k, len(bits))
    out = 0
    for i in bits[::len(bits) // k][:k]:
        out |= 1 << i
    return out


def _count(mask):
    return bin(mask).count("1")


def rank_program(g, core, T, topo):
    rank = T.rank_of(core)
    if rank is None:
        return
    cores = list(T.cores)
    n = len(cores)
    S = T.sem

    def writer(s):
        src, dst = cores[s], cores[(s + 1) % n]
        if topo.may_write(src, dst):
            return src
        return [c for c in cores if c != src and c != dst and topo.chip(c) == topo.chip(src)
                and topo.may_write(c, dst)][0]

    def land_mask(c):
        m = None
        for s in range(n):
            if writer(s) == c:
                e = topo.mask(c, cores[(s + 1) % n])
                m = e if m is None else m & e
        return _pick(m, K_LAND)

    def send(out_ap, in_ap, dst, sem, mask):
        rid, pid, _ = topo.addr(dst)
        g.remote_dma(out_ap, in_ap, sem, S.sent, pid, rid, mask)
        return _count(mask)

    direct = writer(rank) == core
    passes = [s for s in range(n) if s != rank and writer(s) == core]

    if not direct:
        g.sync.dma_start(T.xd[:], T.x[:]).then_inc(S.ldd, 16)
    g.sync.dma_start(T.xs[:], T.x[:]).then_inc(S.ldx, 16)
    g.sync.dma_start(T.ws[:], T.w[:]).then_inc(S.ldw, 16)

    left = 0
    if direct:
        g.wait_ge(S.ldx, 16)
        left += send(T.xp[:], T.xs[:], cores[(rank + 1) % n], S.arr, land_mask(core))
    else:
        g.wait_ge(S.ldd, 16)
        w_core = writer(rank)
        left += send(T.xr[:], T.xd[:], w_core, S.hand, _pick(topo.mask(core, w_core), K_HAND))
    for s in passes:
        g.wait_ge(S.hand, _count(_pick(topo.mask(cores[s], core), K_HAND)))
        left += send(T.xp[:], T.xr[:], cores[(s + 1) % n], S.arr, land_mask(core))
    g.wait_ge(S.sent, left)

    def table(x_buf, outs, sems):
        for u in range(HT):
            for t in range(KT):
                c = 128 * (HT * t + u)
                mm = g.tensor.matmul(outs[u], T.ws[:, c:c + 128], x_buf[:, TK * t:TK * t + TK],
                                     start=(t == 0), stop=(t == KT - 1))
            mm.then_inc(sems[u], 1)

    g.tensor.wait_ge(S.ldx, 16)
    g.tensor.wait_ge(S.ldw, 16)
    table(T.xs, [T.po[:, 0:TK], T.po[:, TK:2 * TK]], [S.po_done, S.po_done])
    g.tensor.wait_ge(S.arr, _count(land_mask(writer((rank - 1) % n))))
    table(T.xp, [T.pp0[:, 0:TK], T.pp1[:, 0:TK]], [S.pp0_done, S.pp1_done])
    g.tensor.wait_ge(S.hr_done, 1)
    g.tensor.wait_ge(S.hp0_done, 1)
    g.tensor.matmul(T.py[0:TK, 0:TK], T.hp[:, 0:TK], T.hr[:, 0:TK], start=True, stop=False)
    g.tensor.wait_ge(S.hp1_done, 1)
    g.tensor.matmul(T.py[0:TK, 0:TK], T.hp[:, TK:2 * TK], T.hr[:, TK:2 * TK],
                    start=False, stop=True).then_inc(S.py_done, 1)

    g.vector.memset(T.zero[:], 0.0).then_inc(S.zs, 1)
    g.vector.wait_ge(S.zs, 1)
    g.vector.wait_ge(S.po_done, HT)
    g.vector.tensor_tensor(T.hr[:], T.po[:, 0:2 * TK], T.zero[:], AluOpType.max).then_inc(S.hr_done, 1)
    g.vector.wait_ge(S.pp0_done, 1)
    g.vector.tensor_tensor(T.hp[:, 0:TK], T.pp0[:, 0:TK], T.zero[:, 0:TK], AluOpType.max).then_inc(S.hp0_done, 1)
    g.vector.wait_ge(S.pp1_done, 1)
    g.vector.tensor_tensor(T.hp[:, TK:2 * TK], T.pp1[:, 0:TK], T.zero[:, 0:TK], AluOpType.max).then_inc(S.hp1_done, 1)
    g.vector.wait_ge(S.py_done, 1)
    g.vector.tensor_copy(T.ys[0:TK, :], T.py[0:TK, 0:TK]).then_inc(S.ys_done, 1)

    g.sync.wait_ge(S.ys_done, 1)
    g.sync.dma_start(T.y[:], T.ys[0:TK, :]).then_inc(S.sty, 16)
    g.sync.wait_ge(S.sty, 16)
